import numpy as np
import ml_dtypes


def mxq(x, axis, fmt="e4m3"):
    dtype, down = {"e4m3": (ml_dtypes.float8_e4m3fn, 7), "e5m2": (ml_dtypes.float8_e5m2, 14)}[fmt]
    v = np.moveaxis(np.asarray(x, np.float32).astype(ml_dtypes.bfloat16).astype(np.float64), axis, -1)
    blocks = v.reshape(v.shape[:-1] + (-1, 32))
    amax = np.abs(blocks).max(-1, keepdims=True)
    byte = np.maximum(np.where(amax > 0, np.frexp(amax)[1] - 1 + 127, 0) - down, 1)
    scale = np.exp2(byte - 127.0)
    codes = (blocks / scale).astype(np.float32).astype(dtype).astype(np.float64)
    return np.moveaxis((codes * scale).reshape(v.shape), -1, axis)


WIDE = False


def mx_kscale(k):
    if not WIDE:
        return np.ones(k)
    levels = np.array([10, -10, 5, -5, 0])
    if k % 512:
        return np.exp2(np.random.permutation(np.resize(levels, k // 32))).repeat(32)
    a = np.empty((k // 512, 16))
    for p in range(k // 512):
        a[p, :8] = np.random.permutation(np.resize(levels, 8))
        for g in range(8):
            far = levels[np.abs(levels - a[p, g]) >= 10]
            a[p, g + 8] = far[np.random.randint(len(far))]
    return np.exp2(a.ravel()).repeat(32)


def f64(x):
    return np.asarray(x).astype(np.float64)


def striped(idx):
    return np.tile(idx.reshape(-1, 16).T, (8, 1)).astype(np.uint16)


def unstriped(offs):
    return offs[:16].T.reshape(-1).astype(np.int64)


E2M1 = np.array([0.0, 0.5, 1.0, 1.5, 2.0, 3.0, 4.0, 6.0, -0.0, -0.5, -1.0, -1.5, -2.0, -3.0, -4.0, -6.0])


def pack_weight(w, fmt):
    k, n = w.shape
    w = f64(np.asarray(w, np.float32).astype(ml_dtypes.bfloat16)).reshape(k // 32, 32, n)
    amax = np.abs(w).max(1)
    if fmt == "e4m3":
        byte = np.frexp(amax)[1] - 1 + 127 - 7
    else:
        mant, ex = np.frexp(amax / 6.0)
        byte = np.where(mant > 0.5, ex, ex - 1) + 127
    byte = np.clip(np.where(amax > 0, byte, 1), 1, 254)
    scaled = (w * np.exp2(127.0 - byte)[:, None, :]).reshape(k, n).astype(np.float32)
    by_word = np.ascontiguousarray(scaled.reshape(k // 512, 128, 4, n).transpose(0, 1, 3, 2))
    if fmt == "e4m3":
        words = by_word.astype(ml_dtypes.float8_e4m3fn).view(np.uint8)
    else:
        c = by_word.astype(ml_dtypes.float4_e2m1fn).view(np.uint8) & 0xF
        words = (c[..., 0::2] | (c[..., 1::2] << 4)).reshape(k // 512, 128, 2 * n)
    return np.ascontiguousarray(words), np.ascontiguousarray(byte.astype(np.uint8).reshape(k // 512, 16, n))


def unpack_weight(words, scales, fmt):
    g, _, n = scales.shape
    words = np.ascontiguousarray(words).reshape(g, 128, n, -1)
    if fmt == "e4m3":
        vals = words.view(ml_dtypes.float8_e4m3fn).astype(np.float64)
    else:
        nib = np.empty((g, 128, n, 4), np.uint8)
        nib[..., 0::2] = words & 0xF
        nib[..., 1::2] = words >> 4
        vals = E2M1[nib]
    vals = vals * np.repeat(np.exp2(scales.astype(np.float64) - 127.0), 8, axis=1)[..., None]
    return vals.transpose(0, 1, 3, 2).reshape(g * 512, n)


def gelu(v):
    return 0.5 * v * (1.0 + np.tanh(np.sqrt(2.0 / np.pi) * (v + 0.044715 * v**3)))


def often(T, S):
    return np.random.permutation(T)[(T * np.random.uniform(0, 1, S) ** 4).astype(np.int64)]


T, S, K, K2, K3, H, P, N = 4096, 1024, 1024, 1536, 512, 512, 512, 384

def setup_inputs():
    n = np.random.standard_normal
    s, s2, s3 = mx_kscale(K)[:, None], mx_kscale(K2)[:, None], mx_kscale(K3)[:, None]
    u = mx_kscale(H)[:, None]
    d = {}
    d["tab_words"], d["tab_scales"] = pack_weight(n((K, T)) * s, "e4m3")
    d["tab2_words"], d["tab2_scales"] = pack_weight(n((K2, T)) * s2, "e4m3")
    d["tab3_words"], d["tab3_scales"] = pack_weight(n((K3, T)) * s3, "e4m3")
    d["offs"] = striped(np.random.permutation(T)[:S])
    d["offs2"] = striped(np.random.permutation(T)[:S])
    d["offs3"] = striped(np.random.permutation(T)[:S])
    d["pos1"] = striped(np.random.permutation(S)[:P])
    d["pos2"] = striped(often(S, P))
    d["pos3"] = striped(often(S, P))
    d["w1"] = (0.7 * n((K, H)) / K**0.5 / s).astype(np.float32)
    d["w2_words"], d["w2_scales"] = pack_weight(0.7 * n((K2, H)) / K2**0.5 / s2, "e2m1")
    d["w3"] = (0.7 * n((K3, H)) / K3**0.5 / s3).astype(np.float32)
    d["gain"] = (np.exp(0.3 * n(H)) * u[:, 0]).astype(np.float32)
    d["w4_words"], d["w4_scales"] = pack_weight(n((H, H)) / H**0.5 / u * u.T, "e4m3")
    d["b4"] = (0.5 * n(H) * u[:, 0]).astype(np.float32)
    d["w5"] = (n((H, N)) / H**0.5 / u).astype(np.float32)
    return d

def reference(tab_words, tab_scales, tab2_words, tab2_scales, tab3_words, tab3_scales, offs, offs2, offs3,
              pos1, pos2, pos3, w1, w2_words, w2_scales, w3, gain, w4_words, w4_scales, b4, w5):
    v = unpack_weight(tab_words, tab_scales, "e4m3")[:, unstriped(offs)]
    v2 = unpack_weight(tab2_words, tab2_scales, "e4m3")[:, unstriped(offs2)]
    v3 = unpack_weight(tab3_words, tab3_scales, "e4m3")[:, unstriped(offs3)]
    a = mxq(f64(w1), 0, "e4m3").T @ v
    b = unpack_weight(w2_words, w2_scales, "e2m1").T @ v2
    d = mxq(f64(w3), 0, "e4m3").T @ v3
    aj = a[:, unstriped(pos1)]
    z = (aj - b[:, unstriped(pos2)]) * (aj - d[:, unstriped(pos3)]) * f64(gain)[:, None]
    y = (unpack_weight(w4_words, w4_scales, "e4m3").T @ mxq(z, 0, "e4m3")) + f64(b4)[:, None]
    h = np.maximum(y, z)
    return mxq(f64(w5), 0, "e4m3").T @ mxq(h, 0, "e4m3")

@@ -1,0 +1,310 @@
+from contextlib import ExitStack
+
+import concourse.mybir as mybir
+
+T, S, H, J, N_OUT = 4096, 1024, 512, 512, 384
+FLOPS = 2 * H * S * (1024 + 1536 + 512) + 2 * H * H * J + 2 * H * N_OUT * J
+
+F32 = mybir.dt.float32
+BF16 = mybir.dt.bfloat16
+I32 = mybir.dt.int32
+U32 = mybir.dt.uint32
+U16 = mybir.dt.uint16
+U8 = mybir.dt.uint8
+FP8X4 = mybir.dt.float8_e4m3fn_x4
+FP4X4 = mybir.dt.float4_e2m1fn_x4
+ALU = mybir.AluOpType
+
+P = 128
+PACK = 4
+HALF = 512
+PIECES = ((0, 256), (256, 256))
+
+
+def tile_list_cell_sharing_scores_kernel(
+    tc, tab_words, tab_scales, tab2_words, tab2_scales, tab3_words, tab3_scales, offs, offs2, offs3,
+    pos1, pos2, pos3, w1, w2_words, w2_scales, w3, gain, w4_words, w4_scales, b4, w5, out,
+):
+    nc = tc.nc
+    with ExitStack() as ctx:
+        keep = ctx.enter_context(tc.tile_pool(name="keep", bufs=1))
+        ring = ctx.enter_context(tc.tile_pool(name="ring", bufs=1))
+        psum = ctx.enter_context(tc.psum_pool(name="psum", bufs=8))
+
+        def load_list(src, name):
+            lst = keep.tile([P, src.shape[1]], U16, name=name)
+            nc.sync.dma_start(lst[:], src)
+            return lst
+
+        def zeroed_bytes(width, name):
+            plane = keep.tile([P, width], U8, name=name, align_bytes=64)
+            nc.vector.memset(plane[:].bitcast(I32), 0)
+            return plane
+
+        def load_table_scales(window, scales):
+            rows = 4 * scales.shape[0]
+            for q in range(4):
+                nc.gpsimd.dma_start(
+                    window[32 * q : 32 * q + rows, :].bitcast(I32), scales[:, 4 * q : 4 * q + 4, :].bitcast(I32)
+                )
+
+        def load_weight_scales(planes, first, scales):
+            passes = scales.shape[0]
+            for q in range(4):
+                nc.sync.dma_start(
+                    planes[32 * q : 32 * q + 4, first * H : (first + passes) * H]
+                    .bitcast(I32)
+                    .rearrange("r (a c) -> r a c", a=passes),
+                    scales[:, 4 * q : 4 * q + 4, :].bitcast(I32).rearrange("a r c -> r a c"),
+                )
+
+        def load_table_pass(words, a, name):
+            window = ring.tile([P, T], I32, tag="table", bufs=5, name=name)
+            nc.sync.dma_start(window[:], words[a].rearrange("p t i -> p (t i)").bitcast(I32))
+            return window
+
+        def load_rows(rows, name):
+            width = rows.shape[1]
+            raw = ring.tile([P, PACK, width], F32, tag="raw", bufs=3, name=name)
+            nc.sync.dma_start(raw[:], rows.rearrange("(p j) c -> p j c", j=PACK))
+            return raw
+
+        def gather_scales(window, lst, name):
+            picked = keep.tile([P, S], U8, name=name, align_bytes=64)
+            nc.vector.tensor_copy(picked[:], window[:].indirect(lst[:]))
+            return picked
+
+        def gather_words(window, lst, half, name):
+            picked = ring.tile([P, HALF], U32, tag="picked", bufs=8, name=name, align_bytes=64)
+            cols = HALF // 16
+            nc.vector.tensor_copy(picked[:], window[:].bitcast(U32).indirect(lst[:, half * cols : (half + 1) * cols]))
+            return picked
+
+        def weave_dealt(mover, raw, name):
+            woven = ring.tile([P, PACK * H], BF16, tag="woven", bufs=2, name=name, align_bytes=64)
+            mover(
+                woven[:].rearrange("p (t m j) -> p m j t", t=PACK, j=PACK),
+                raw[:].rearrange("p j (m t) -> p m j t", t=PACK),
+            )
+            return woven
+
+        def weave(mover, planes, width, name):
+            woven = ring.tile([P, PACK * width], BF16, tag="woven", bufs=2, name=name, align_bytes=64)
+            mover(
+                woven[:].rearrange("p (c i t) -> p c t i", t=PACK, i=4),
+                planes.rearrange("p t (c i) -> p c t i", i=4),
+            )
+            return woven
+
+        def quantize(woven, width, name):
+            codes = keep.tile([P, width], U32, name=name + "_codes", align_bytes=64)
+            scales = keep.tile([P, width], U8, name=name + "_scales", align_bytes=64)
+            nc.vector.quantize_mx(out=codes[:].bitcast(FP8X4), scales=scales[:], in_=woven[:])
+            return codes, scales
+
+        def new_banks(name):
+            return [[psum.tile([P, HALF], F32, tag="bank", name="%s%d%d" % (name, t, h)) for h in range(2)] for t in range(PACK)]
+
+        def new_results(name):
+            return [ring.tile([P, S], F32, tag="result", bufs=8, name="%s%d" % (name, t)) for t in range(PACK)]
+
+        def first_stage_pass(banks, half, lhs, lhs_scales, picked, picked_scales, start, stop):
+            for t in range(PACK):
+                nc.tensor.matmul_mx(
+                    out=banks[t][half][:],
+                    lhsT=lhs(t),
+                    lhsT_scale=lhs_scales[:, t * P : (t + 1) * P],
+                    rhs=picked[:].bitcast(FP8X4),
+                    rhs_scale=picked_scales[:, half * HALF : (half + 1) * HALF],
+                    start=start,
+                    stop=stop,
+                )
+
+        def empty_bank(mover, results, banks, t, half):
+            mover(results[t][:, half * HALF : (half + 1) * HALF], banks[t][half][:])
+
+        EMPTY_ORDER = ((0, 0), (1, 0), (0, 1), (1, 1), (2, 0), (2, 1), (3, 0), (3, 1))
+
+        win_a = zeroed_bytes(T, "win_a")
+        win_d = zeroed_bytes(T, "win_d")
+        win_b = zeroed_bytes(T, "win_b")
+        ws_raw = zeroed_bytes(4 * H, "ws_raw")
+        sb_moved = zeroed_bytes(2 * S, "sb_moved")
+        load_table_scales(win_a, tab_scales)
+        load_table_scales(win_d, tab3_scales)
+        load_table_scales(win_b, tab2_scales)
+
+        l_a = load_list(offs, "l_a")
+        w1_raw = [load_rows(w1[0:512, :], "w1_raw0")]
+        tab_a0 = load_table_pass(tab_words, 0, "tab_a0")
+        l_d = load_list(offs3, "l_d")
+        l_b = load_list(offs2, "l_b")
+        w1_raw.append(load_rows(w1[512:1024, :], "w1_raw1"))
+        p_a = load_list(pos1, "p_a")
+        tab_a1 = load_table_pass(tab_words, 1, "tab_a1")
+        w3_raw = load_rows(w3, "w3_raw")
+        load_weight_scales(ws_raw, 3, w4_scales)
+        tab_d = load_table_pass(tab3_words, 0, "tab_d")
+        load_weight_scales(ws_raw, 0, w2_scales)
+        p_d = load_list(pos3, "p_d")
+        w2_raw = keep.tile([P, 3, 2 * H], U8, name="w2_raw")
+        nc.sync.dma_start(w2_raw[:].bitcast(I32), w2_words.bitcast(I32).rearrange("a p c -> p a c"))
+        tab_b = [load_table_pass(tab2_words, 0, "tab_b0")]
+        gain_t = keep.tile([P, PACK], F32, name="gain_t")
+        nc.sync.dma_start(gain_t[:], gain.rearrange("(p t) -> p t", t=PACK))
+        b4_t = keep.tile([P, PACK], F32, name="b4_t")
+        nc.sync.dma_start(b4_t[:], b4.rearrange("(p t) -> p t", t=PACK))
+        p_b = load_list(pos2, "p_b")
+        tab_b.append(load_table_pass(tab2_words, 1, "tab_b1"))
+
+        s_a = gather_scales(win_a, l_a, "s_a")
+        w1_q = [quantize(weave_dealt(nc.scalar.copy, w1_raw[0], "w1_woven0"), H, "w1_0")]
+        g_a0 = [gather_words(tab_a0, l_a, h, "g_a0%d" % h) for h in range(2)]
+        tab_b.append(load_table_pass(tab2_words, 2, "tab_b2"))
+        w4_raw = keep.tile([P, H], I32, name="w4_raw")
+        nc.sync.dma_start(w4_raw[:], w4_words[0].rearrange("p c i -> p (c i)").bitcast(I32))
+        w5_raw = load_rows(w5, "w5_raw")
+        s_d = gather_scales(win_d, l_d, "s_d")
+        w1_q.append(quantize(weave_dealt(nc.scalar.copy, w1_raw[1], "w1_woven1"), H, "w1_1"))
+        s_b = gather_scales(win_b, l_b, "s_b")
+        for a in (1, 2):
+            nc.gpsimd.dma_start(
+                sb_moved[0:112, (a - 1) * S : a * S].bitcast(I32), s_b[4 * a : 4 * a + 112, :].bitcast(I32)
+            )
+
+        def e4m3_columns(codes):
+            return lambda t: codes[:, t * P : (t + 1) * P].bitcast(FP8X4)
+
+        banks = new_banks("acc_a")
+        for h in range(2):
+            first_stage_pass(banks, h, e4m3_columns(w1_q[0][0]), w1_q[0][1], g_a0[h], s_a, True, False)
+        for h in range(2):
+            picked = gather_words(tab_a1, l_a, h, "g_a1%d" % h)
+            first_stage_pass(banks, h, e4m3_columns(w1_q[1][0]), w1_q[1][1], picked, s_a[4:P, :], False, True)
+        w3_woven = weave_dealt(nc.vector.tensor_copy, w3_raw, "w3_woven")
+        res_a = new_results("a")
+        for t, h in EMPTY_ORDER:
+            empty_bank(nc.scalar.copy, res_a, banks, t, h)
+        aj = keep.tile([P, PACK, J], F32, name="aj")
+        nc.vector.tensor_copy(aj[:, 0, :], res_a[0][:].indirect(p_a[:]))
+        w3_q = quantize(w3_woven, H, "w3")
+        for t in range(1, PACK):
+            nc.vector.tensor_copy(aj[:, t, :], res_a[t][:].indirect(p_a[:]))
+
+        banks = new_banks("acc_d")
+        for h in range(2):
+            picked = gather_words(tab_d, l_d, h, "g_d%d" % h)
+            first_stage_pass(banks, h, e4m3_columns(w3_q[0]), w3_q[1], picked, s_d, True, True)
+        ws = keep.tile([P, 4 * H], U8, name="ws", align_bytes=64)
+        nc.vector.tensor_copy(
+            ws[:].rearrange("p (a t m) -> p a t m", a=4, t=PACK), ws_raw[:].rearrange("p (a m t) -> p a t m", a=4, t=PACK)
+        )
+        res_d = new_results("d")
+        for t, h in EMPTY_ORDER:
+            empty_bank(nc.scalar.copy, res_d, banks, t, h)
+        w2 = keep.tile([P, 3 * 2 * H], U8, name="w2", align_bytes=64)
+        nc.scalar.copy(
+            w2[:].bitcast(U16).rearrange("p (a t m) -> p a t m", a=3, t=PACK),
+            w2_raw[:].bitcast(U16).rearrange("p a (m t) -> p a t m", t=PACK),
+        )
+
+        def e2m1_columns(a):
+            return lambda t: w2[:, (a * H + t * P) * 2 : (a * H + (t + 1) * P) * 2].bitcast(FP4X4)
+
+        s_b_planes = [s_b, sb_moved[:, 0:S], sb_moved[:, S : 2 * S]]
+        da = keep.tile([P, PACK, J], F32, name="da")
+        banks = new_banks("acc_b")
+        for a in range(3):
+            for h in range(2):
+                picked = gather_words(tab_b[a], l_b, h, "g_b%d%d" % (a, h))
+                first_stage_pass(
+                    banks, h, e2m1_columns(a), ws[:, a * H : (a + 1) * H], picked, s_b_planes[a], a == 0, a == 2
+                )
+            if a < 2:
+                for t in (2 * a, 2 * a + 1):
+                    nc.vector.tensor_tensor(da[:, t, :], res_d[t][:].indirect(p_d[:]), aj[:, t, :], ALU.subtract)
+        res_b = new_results("b")
+        for t, h in EMPTY_ORDER:
+            empty_bank(nc.vector.tensor_copy if (h == 0 and t >= 2) else nc.scalar.copy, res_b, banks, t, h)
+        w4 = keep.tile([P, H], U32, name="w4", align_bytes=64)
+        nc.scalar.copy(
+            w4[:].rearrange("p (t m) -> p m t", t=PACK), w4_raw[:].bitcast(U32).rearrange("p (m t) -> p m t", t=PACK)
+        )
+
+        z = keep.tile([P, PACK, J], F32, name="z")
+
+        def join(first, width):
+            cols = slice(first, first + width)
+            offsets = p_b[:, first // 16 : (first + width) // 16]
+            diffs = []
+
+            def product(t):
+                nc.vector.scalar_tensor_tensor(
+                    z[:, t, cols], diffs[t][:], gain_t[:, t : t + 1], da[:, t, cols], ALU.mult, ALU.mult
+                )
+
+            for t in range(PACK):
+                ba = ring.tile([P, width], F32, tag="ba", bufs=3, name="ba%d_%d" % (first, t))
+                nc.vector.tensor_tensor(ba[:], res_b[t][:].indirect(offsets), aj[:, t, cols], ALU.subtract)
+                diffs.append(ba)
+                if t > 0:
+                    product(t - 1)
+            product(PACK - 1)
+            return weave(nc.scalar.copy, z[:, :, cols], width, "z_woven%d" % first)
+
+        def hidden(first, width, z_woven):
+            cols = slice(first, first + width)
+            codes, scales = quantize(z_woven, width, "z%d" % first)
+            ys = []
+            for t in range(PACK):
+                y = psum.tile([P, width], F32, tag="bank", name="y%d_%d" % (first, t))
+                nc.tensor.matmul_mx(
+                    out=y[:],
+                    lhsT=w4[:, t * P : (t + 1) * P].bitcast(FP8X4),
+                    lhsT_scale=ws[:, 3 * H + t * P : 3 * H + (t + 1) * P],
+                    rhs=codes[:].bitcast(FP8X4),
+                    rhs_scale=scales[:],
+                    start=True,
+                    stop=True,
+                )
+                ys.append(y)
+            return ys
+
+        def larger(first, width, ys):
+            cols = slice(first, first + width)
+            hid = ring.tile([P, PACK, width], F32, tag="result", bufs=8, name="h%d" % first)
+            for t in range(PACK):
+                nc.vector.scalar_tensor_tensor(hid[:, t, :], ys[t][:], b4_t[:, t : t + 1], z[:, t, cols], ALU.add, ALU.max)
+            return weave(nc.scalar.copy, hid[:], width, "h_woven%d" % first)
+
+        def scores(first, width, h_woven, w5_q, last):
+            codes, scales = quantize(h_woven, width, "h%d" % first)
+            staged = ring.tile([P, N_OUT // P, width], F32, tag="result", bufs=8, name="staged%d" % first)
+            for n in range(N_OUT // P):
+                acc = psum.tile([P, width], F32, tag="bank", name="o%d_%d" % (first, n))
+                nc.tensor.matmul_mx(
+                    out=acc[:],
+                    lhsT=w5_q[0][:, n * P : (n + 1) * P].bitcast(FP8X4),
+                    lhsT_scale=w5_q[1][:, n * P : (n + 1) * P],
+                    rhs=codes[:].bitcast(FP8X4),
+                    rhs_scale=scales[:],
+                    start=True,
+                    stop=True,
+                )
+                mover = nc.vector.tensor_copy if (last and n == 1) else nc.scalar.copy
+                mover(staged[:, n, :], acc[:])
+            nc.sync.dma_start(out.rearrange("(n p) j -> p n j", p=P)[:, :, first : first + width], staged[:])
+
+        z0 = join(*PIECES[0])
+        w5_woven = keep.tile([P, PACK * N_OUT], BF16, name="w5_woven", align_bytes=64)
+        nc.scalar.copy(
+            w5_woven[:].rearrange("p (c i t) -> p c t i", t=PACK, i=4), w5_raw[:].rearrange("p t (c i) -> p c t i", i=4)
+        )
+        y0 = hidden(*PIECES[0], z0)
+        z1 = join(*PIECES[1])
+        h0 = larger(*PIECES[0], y0)
+        w5_q = quantize(w5_woven, N_OUT, "w5")
+        y1 = hidden(*PIECES[1], z1)
+        scores(*PIECES[0], h0, w5_q, False)
+        h1 = larger(*PIECES[1], y1)
+        scores(*PIECES[1], h1, w5_q, True)

@@ -41,12 +41,18 @@ def tile_list_cell_sharing_scores_kernel(
             nc.vector.memset(plane[:].bitcast(I32), 0)
             return plane
 
-        def load_table_scales(window, scales):
-            rows = 4 * scales.shape[0]
-            for q in range(4):
-                nc.gpsimd.dma_start(
-                    window[32 * q : 32 * q + rows, :].bitcast(I32), scales[:, 4 * q : 4 * q + 4, :].bitcast(I32)
-                )
+        def load_two_passes_scales(window, scales, r):
+            nc.sync.dma_start(
+                window[r:P:16, :].bitcast(I32), scales[0:2, r:16:4, :].bitcast(I32).rearrange("a q t -> q a t")
+            )
+
+        def load_one_pass_scales(window, first, scales, q):
+            nc.sync.dma_start(
+                window[32 * q + first : 32 * q + first + 4, :].bitcast(I32), scales[4 * q : 4 * q + 4, :].bitcast(I32)
+            )
+
+        def move_up(plane, picked, first):
+            nc.sync.dma_start(plane[0:112, :].bitcast(I32), picked[first : first + 112, :].bitcast(I32))
 
         def load_weight_scales(planes, first, scales):
             passes = scales.shape[0]
@@ -129,35 +135,45 @@ def tile_list_cell_sharing_scores_kernel(
         win_d = zeroed_bytes(T, "win_d")
         win_b = zeroed_bytes(T, "win_b")
         ws_raw = zeroed_bytes(4 * H, "ws_raw")
-        sb_moved = zeroed_bytes(2 * S, "sb_moved")
-        load_table_scales(win_a, tab_scales)
-        load_table_scales(win_d, tab3_scales)
-        load_table_scales(win_b, tab2_scales)
+        s_a1 = zeroed_bytes(S, "s_a1")
+        s_b1 = zeroed_bytes(S, "s_b1")
+        s_b2 = zeroed_bytes(S, "s_b2")
 
         l_a = load_list(offs, "l_a")
-        w1_raw = [load_rows(w1[0:512, :], "w1_raw0")]
-        tab_a0 = load_table_pass(tab_words, 0, "tab_a0")
         l_d = load_list(offs3, "l_d")
         l_b = load_list(offs2, "l_b")
-        w1_raw.append(load_rows(w1[512:1024, :], "w1_raw1"))
         p_a = load_list(pos1, "p_a")
+        p_d = load_list(pos3, "p_d")
+        p_b = load_list(pos2, "p_b")
+        gain_t = keep.tile([P, PACK], F32, name="gain_t")
+        nc.sync.dma_start(gain_t[:], gain.rearrange("(p t) -> p t", t=PACK))
+        w1_raw = [load_rows(w1[0:512, :], "w1_raw0")]
+        for r in range(4):
+            load_two_passes_scales(win_a, tab_scales, r)
+        tab_a0 = load_table_pass(tab_words, 0, "tab_a0")
+        for q in range(4):
+            load_one_pass_scales(win_d, 0, tab3_scales[0], q)
+        for r in range(2):
+            load_two_passes_scales(win_b, tab2_scales, r)
+        w1_raw.append(load_rows(w1[512:1024, :], "w1_raw1"))
+        for r in range(2, 4):
+            load_two_passes_scales(win_b, tab2_scales, r)
+        for q in range(4):
+            load_one_pass_scales(win_b, 8, tab2_scales[2], q)
         tab_a1 = load_table_pass(tab_words, 1, "tab_a1")
+        load_weight_scales(ws_raw, 0, w2_scales)
+        tab_d = load_table_pass(tab3_words, 0, "tab_d")
         w3_raw = load_rows(w3, "w3_raw")
         load_weight_scales(ws_raw, 3, w4_scales)
-        tab_d = load_table_pass(tab3_words, 0, "tab_d")
-        load_weight_scales(ws_raw, 0, w2_scales)
-        p_d = load_list(pos3, "p_d")
         w2_raw = keep.tile([P, 3, 2 * H], U8, name="w2_raw")
         nc.sync.dma_start(w2_raw[:].bitcast(I32), w2_words.bitcast(I32).rearrange("a p c -> p a c"))
         tab_b = [load_table_pass(tab2_words, 0, "tab_b0")]
-        gain_t = keep.tile([P, PACK], F32, name="gain_t")
-        nc.sync.dma_start(gain_t[:], gain.rearrange("(p t) -> p t", t=PACK))
         b4_t = keep.tile([P, PACK], F32, name="b4_t")
         nc.sync.dma_start(b4_t[:], b4.rearrange("(p t) -> p t", t=PACK))
-        p_b = load_list(pos2, "p_b")
         tab_b.append(load_table_pass(tab2_words, 1, "tab_b1"))
 
         s_a = gather_scales(win_a, l_a, "s_a")
+        move_up(s_a1, s_a, 16)
         w1_q = [quantize(weave_dealt(nc.scalar.copy, w1_raw[0], "w1_woven0"), H, "w1_0")]
         g_a0 = [gather_words(tab_a0, l_a, h, "g_a0%d" % h) for h in range(2)]
         tab_b.append(load_table_pass(tab2_words, 2, "tab_b2"))
@@ -167,10 +183,8 @@ def tile_list_cell_sharing_scores_kernel(
         s_d = gather_scales(win_d, l_d, "s_d")
         w1_q.append(quantize(weave_dealt(nc.scalar.copy, w1_raw[1], "w1_woven1"), H, "w1_1"))
         s_b = gather_scales(win_b, l_b, "s_b")
-        for a in (1, 2):
-            nc.gpsimd.dma_start(
-                sb_moved[0:112, (a - 1) * S : a * S].bitcast(I32), s_b[4 * a : 4 * a + 112, :].bitcast(I32)
-            )
+        move_up(s_b1, s_b, 16)
+        move_up(s_b2, s_b, 8)
 
         def e4m3_columns(codes):
             return lambda t: codes[:, t * P : (t + 1) * P].bitcast(FP8X4)
@@ -180,25 +194,30 @@ def tile_list_cell_sharing_scores_kernel(
             first_stage_pass(banks, h, e4m3_columns(w1_q[0][0]), w1_q[0][1], g_a0[h], s_a, True, False)
         for h in range(2):
             picked = gather_words(tab_a1, l_a, h, "g_a1%d" % h)
-            first_stage_pass(banks, h, e4m3_columns(w1_q[1][0]), w1_q[1][1], picked, s_a[4:P, :], False, True)
-        w3_woven = weave_dealt(nc.vector.tensor_copy, w3_raw, "w3_woven")
+            first_stage_pass(banks, h, e4m3_columns(w1_q[1][0]), w1_q[1][1], picked, s_a1, False, True)
+        ws = keep.tile([P, 4 * H], U8, name="ws", align_bytes=64)
+
+        def deal_scales(first, passes):
+            cols = slice(first * H, (first + passes) * H)
+            nc.vector.tensor_copy(
+                ws[:, cols].rearrange("p (a t m) -> p a t m", a=passes, t=PACK),
+                ws_raw[:, cols].rearrange("p (a m t) -> p a t m", a=passes, t=PACK),
+            )
+
+        deal_scales(0, 3)
         res_a = new_results("a")
         for t, h in EMPTY_ORDER:
             empty_bank(nc.scalar.copy, res_a, banks, t, h)
         aj = keep.tile([P, PACK, J], F32, name="aj")
-        nc.vector.tensor_copy(aj[:, 0, :], res_a[0][:].indirect(p_a[:]))
-        w3_q = quantize(w3_woven, H, "w3")
-        for t in range(1, PACK):
+        for t in range(PACK):
             nc.vector.tensor_copy(aj[:, t, :], res_a[t][:].indirect(p_a[:]))
 
         banks = new_banks("acc_d")
+        g_d = [gather_words(tab_d, l_d, h, "g_d%d" % h) for h in range(2)]
+        w3_q = quantize(weave_dealt(nc.scalar.copy, w3_raw, "w3_woven"), H, "w3")
         for h in range(2):
-            picked = gather_words(tab_d, l_d, h, "g_d%d" % h)
-            first_stage_pass(banks, h, e4m3_columns(w3_q[0]), w3_q[1], picked, s_d, True, True)
-        ws = keep.tile([P, 4 * H], U8, name="ws", align_bytes=64)
-        nc.vector.tensor_copy(
-            ws[:].rearrange("p (a t m) -> p a t m", a=4, t=PACK), ws_raw[:].rearrange("p (a m t) -> p a t m", a=4, t=PACK)
-        )
+            first_stage_pass(banks, h, e4m3_columns(w3_q[0]), w3_q[1], g_d[h], s_d, True, True)
+        deal_scales(3, 1)
         res_d = new_results("d")
         for t, h in EMPTY_ORDER:
             empty_bank(nc.scalar.copy, res_d, banks, t, h)
@@ -211,7 +230,7 @@ def tile_list_cell_sharing_scores_kernel(
         def e2m1_columns(a):
             return lambda t: w2[:, (a * H + t * P) * 2 : (a * H + (t + 1) * P) * 2].bitcast(FP4X4)
 
-        s_b_planes = [s_b, sb_moved[:, 0:S], sb_moved[:, S : 2 * S]]
+        s_b_planes = [s_b, s_b1, s_b2]
         da = keep.tile([P, PACK, J], F32, name="da")
         banks = new_banks("acc_b")
         for a in range(3):
@@ -270,12 +289,12 @@ def tile_list_cell_sharing_scores_kernel(
                 ys.append(y)
             return ys
 
-        def larger(first, width, ys):
+        def larger(first, width, ys, mover):
             cols = slice(first, first + width)
             hid = ring.tile([P, PACK, width], F32, tag="result", bufs=8, name="h%d" % first)
             for t in range(PACK):
                 nc.vector.scalar_tensor_tensor(hid[:, t, :], ys[t][:], b4_t[:, t : t + 1], z[:, t, cols], ALU.add, ALU.max)
-            return weave(nc.scalar.copy, hid[:], width, "h_woven%d" % first)
+            return weave(mover, hid[:], width, "h_woven%d" % first)
 
         def scores(first, width, h_woven, w5_q, last):
             codes, scales = quantize(h_woven, width, "h%d" % first)
@@ -302,9 +321,9 @@ def tile_list_cell_sharing_scores_kernel(
         )
         y0 = hidden(*PIECES[0], z0)
         z1 = join(*PIECES[1])
-        h0 = larger(*PIECES[0], y0)
+        h0 = larger(*PIECES[0], y0, nc.scalar.copy)
         w5_q = quantize(w5_woven, N_OUT, "w5")
         y1 = hidden(*PIECES[1], z1)
         scores(*PIECES[0], h0, w5_q, False)
-        h1 = larger(*PIECES[1], y1)
+        h1 = larger(*PIECES[1], y1, nc.vector.tensor_copy)
         scores(*PIECES[1], h1, w5_q, True)

@@ -36,36 +36,32 @@ def tile_list_cell_sharing_scores_kernel(
             nc.sync.dma_start(lst[:], src)
             return lst
 
-        def zeroed_bytes(width, name):
+        def zeroed_bytes(engine, width, name):
             plane = keep.tile([P, width], U8, name=name, align_bytes=64)
-            nc.vector.memset(plane[:].bitcast(I32), 0)
+            engine.memset(plane[:].bitcast(I32), 0)
             return plane
 
-        def load_two_passes_scales(window, scales, r):
-            nc.sync.dma_start(
-                window[r:P:16, :].bitcast(I32), scales[0:2, r:16:4, :].bitcast(I32).rearrange("a q t -> q a t")
-            )
+        def load_packed_scales(queue, window, first, scales):
+            rows = 4 * scales.shape[0]
+            for q in range(4):
+                queue.dma_start(
+                    window[32 * q + first : 32 * q + first + rows, :].bitcast(I32),
+                    scales[:, 4 * q : 4 * q + 4, :].bitcast(I32),
+                )
 
-        def load_one_pass_scales(window, first, scales, q):
-            nc.sync.dma_start(
-                window[32 * q + first : 32 * q + first + 4, :].bitcast(I32), scales[4 * q : 4 * q + 4, :].bitcast(I32)
-            )
+        def load_scales_side_by_side(queue, planes, first, scales):
+            passes = scales.shape[0]
+            for r in range(4):
+                queue.dma_start(
+                    planes[first + r : P : 32].bitcast(I32).rearrange("q (a c) -> q a c", a=passes),
+                    scales[:, r:16:4, :].bitcast(I32).rearrange("a q c -> q a c"),
+                )
 
         def move_up(plane, picked, first):
             nc.sync.dma_start(plane[0:112, :].bitcast(I32), picked[first : first + 112, :].bitcast(I32))
 
-        def load_weight_scales(planes, first, scales):
-            passes = scales.shape[0]
-            for q in range(4):
-                nc.sync.dma_start(
-                    planes[32 * q : 32 * q + 4, first * H : (first + passes) * H]
-                    .bitcast(I32)
-                    .rearrange("r (a c) -> r a c", a=passes),
-                    scales[:, 4 * q : 4 * q + 4, :].bitcast(I32).rearrange("a r c -> r a c"),
-                )
-
         def load_table_pass(words, a, name):
-            window = ring.tile([P, T], I32, tag="table", bufs=5, name=name)
+            window = ring.tile([P, T], I32, tag="table", bufs=3, name=name)
             nc.sync.dma_start(window[:], words[a].rearrange("p t i -> p (t i)").bitcast(I32))
             return window
 
@@ -80,22 +76,23 @@ def tile_list_cell_sharing_scores_kernel(
             nc.vector.tensor_copy(picked[:], window[:].indirect(lst[:]))
             return picked
 
-        def gather_words(window, lst, half, name):
-            picked = ring.tile([P, HALF], U32, tag="picked", bufs=8, name=name, align_bytes=64)
-            cols = HALF // 16
-            nc.vector.tensor_copy(picked[:], window[:].bitcast(U32).indirect(lst[:, half * cols : (half + 1) * cols]))
+        def gather_words(window, lst, first, count, name, tag, bufs):
+            picked = ring.tile([P, count], U32, tag=tag, bufs=bufs, name=name, align_bytes=64)
+            nc.vector.tensor_copy(
+                picked[:], window[:].bitcast(U32).indirect(lst[:, first // 16 : (first + count) // 16])
+            )
             return picked
 
-        def weave_dealt(mover, raw, name):
+        def weave_dealt(raw, name):
             woven = ring.tile([P, PACK * H], BF16, tag="woven", bufs=2, name=name, align_bytes=64)
-            mover(
-                woven[:].rearrange("p (t m j) -> p m j t", t=PACK, j=PACK),
-                raw[:].rearrange("p j (m t) -> p m j t", t=PACK),
+            nc.scalar.copy(
+                woven[:].rearrange("p (u e m j) -> p u m j e", u=2, e=2, j=PACK),
+                raw[:].rearrange("p j (m u e) -> p u m j e", u=2, e=2),
             )
             return woven
 
-        def weave(mover, planes, width, name):
-            woven = ring.tile([P, PACK * width], BF16, tag="woven", bufs=2, name=name, align_bytes=64)
+        def weave(mover, planes, width, name, tag):
+            woven = ring.tile([P, PACK * width], BF16, tag=tag, bufs=1, name=name, align_bytes=64)
             mover(
                 woven[:].rearrange("p (c i t) -> p c t i", t=PACK, i=4),
                 planes.rearrange("p t (c i) -> p c t i", i=4),
@@ -111,33 +108,38 @@ def tile_list_cell_sharing_scores_kernel(
         def new_banks(name):
             return [[psum.tile([P, HALF], F32, tag="bank", name="%s%d%d" % (name, t, h)) for h in range(2)] for t in range(PACK)]
 
-        def new_results(name):
-            return [ring.tile([P, S], F32, tag="result", bufs=8, name="%s%d" % (name, t)) for t in range(PACK)]
+        def new_results(name, tag):
+            return [ring.tile([P, S], F32, tag="%s%d" % (tag, t), bufs=1, name="%s%d" % (name, t), align_bytes=64) for t in range(PACK)]
 
-        def first_stage_pass(banks, half, lhs, lhs_scales, picked, picked_scales, start, stop):
-            for t in range(PACK):
+        def first_stage_pass(banks, lhs, lhs_scales, picked, picked_scales, start, stop):
+            for t, half in EMPTY_ORDER:
                 nc.tensor.matmul_mx(
                     out=banks[t][half][:],
                     lhsT=lhs(t),
                     lhsT_scale=lhs_scales[:, t * P : (t + 1) * P],
-                    rhs=picked[:].bitcast(FP8X4),
+                    rhs=picked[half].bitcast(FP8X4),
                     rhs_scale=picked_scales[:, half * HALF : (half + 1) * HALF],
                     start=start,
                     stop=stop,
                 )
 
-        def empty_bank(mover, results, banks, t, half):
-            mover(results[t][:, half * HALF : (half + 1) * HALF], banks[t][half][:])
+        def halves(picked):
+            return [picked[:, 0:HALF], picked[:, HALF:S]]
+
+        def empty_bank(results, banks, t, half):
+            nc.scalar.copy(results[t][:, half * HALF : (half + 1) * HALF], banks[t][half][:])
 
         EMPTY_ORDER = ((0, 0), (1, 0), (0, 1), (1, 1), (2, 0), (2, 1), (3, 0), (3, 1))
 
-        win_a = zeroed_bytes(T, "win_a")
-        win_d = zeroed_bytes(T, "win_d")
-        win_b = zeroed_bytes(T, "win_b")
-        ws_raw = zeroed_bytes(4 * H, "ws_raw")
-        s_a1 = zeroed_bytes(S, "s_a1")
-        s_b1 = zeroed_bytes(S, "s_b1")
-        s_b2 = zeroed_bytes(S, "s_b2")
+        win_a = zeroed_bytes(nc.vector, T, "win_a")
+        win_d = zeroed_bytes(nc.vector, T, "win_d")
+        win_b = zeroed_bytes(nc.vector, T, "win_b")
+        ws_raw = zeroed_bytes(nc.vector, 4 * H, "ws_raw")
+        s_b1 = zeroed_bytes(nc.vector, S, "s_b1")
+        s_b2 = zeroed_bytes(nc.vector, S, "s_b2")
+
+        load_scales_side_by_side(nc.gpsimd, win_d[:], 12, tab3_scales)
+        load_packed_scales(nc.gpsimd, win_b, 0, tab2_scales)
 
         l_a = load_list(offs, "l_a")
         l_d = load_list(offs3, "l_d")
@@ -147,104 +149,96 @@ def tile_list_cell_sharing_scores_kernel(
         p_b = load_list(pos2, "p_b")
         gain_t = keep.tile([P, PACK], F32, name="gain_t")
         nc.sync.dma_start(gain_t[:], gain.rearrange("(p t) -> p t", t=PACK))
-        w1_raw = [load_rows(w1[0:512, :], "w1_raw0")]
-        for r in range(4):
-            load_two_passes_scales(win_a, tab_scales, r)
         tab_a0 = load_table_pass(tab_words, 0, "tab_a0")
-        for q in range(4):
-            load_one_pass_scales(win_d, 0, tab3_scales[0], q)
-        for r in range(2):
-            load_two_passes_scales(win_b, tab2_scales, r)
+        load_packed_scales(nc.sync, win_a, 4, tab_scales)
+        w1_raw = [load_rows(w1[0:512, :], "w1_raw0")]
         w1_raw.append(load_rows(w1[512:1024, :], "w1_raw1"))
-        for r in range(2, 4):
-            load_two_passes_scales(win_b, tab2_scales, r)
-        for q in range(4):
-            load_one_pass_scales(win_b, 8, tab2_scales[2], q)
         tab_a1 = load_table_pass(tab_words, 1, "tab_a1")
-        load_weight_scales(ws_raw, 0, w2_scales)
-        tab_d = load_table_pass(tab3_words, 0, "tab_d")
+        load_scales_side_by_side(nc.sync, ws_raw[:, 0 : 3 * H], 0, w2_scales)
         w3_raw = load_rows(w3, "w3_raw")
-        load_weight_scales(ws_raw, 3, w4_scales)
-        w2_raw = keep.tile([P, 3, 2 * H], U8, name="w2_raw")
-        nc.sync.dma_start(w2_raw[:].bitcast(I32), w2_words.bitcast(I32).rearrange("a p c -> p a c"))
-        tab_b = [load_table_pass(tab2_words, 0, "tab_b0")]
+        load_scales_side_by_side(nc.sync, ws_raw[:, 3 * H : 4 * H], 0, w4_scales)
+        tab_d = load_table_pass(tab3_words, 0, "tab_d")
         b4_t = keep.tile([P, PACK], F32, name="b4_t")
         nc.sync.dma_start(b4_t[:], b4.rearrange("(p t) -> p t", t=PACK))
-        tab_b.append(load_table_pass(tab2_words, 1, "tab_b1"))
-
-        s_a = gather_scales(win_a, l_a, "s_a")
-        move_up(s_a1, s_a, 16)
-        w1_q = [quantize(weave_dealt(nc.scalar.copy, w1_raw[0], "w1_woven0"), H, "w1_0")]
-        g_a0 = [gather_words(tab_a0, l_a, h, "g_a0%d" % h) for h in range(2)]
-        tab_b.append(load_table_pass(tab2_words, 2, "tab_b2"))
-        w4_raw = keep.tile([P, H], I32, name="w4_raw")
-        nc.sync.dma_start(w4_raw[:], w4_words[0].rearrange("p c i -> p (c i)").bitcast(I32))
-        w5_raw = load_rows(w5, "w5_raw")
-        s_d = gather_scales(win_d, l_d, "s_d")
-        w1_q.append(quantize(weave_dealt(nc.scalar.copy, w1_raw[1], "w1_woven1"), H, "w1_1"))
-        s_b = gather_scales(win_b, l_b, "s_b")
-        move_up(s_b1, s_b, 16)
-        move_up(s_b2, s_b, 8)
+        w2_raw = keep.tile([P, 3, 2 * H], U8, name="w2_raw")
+        nc.sync.dma_start(w2_raw[:].bitcast(I32), w2_words.bitcast(I32).rearrange("a p c -> p a c"))
 
         def e4m3_columns(codes):
             return lambda t: codes[:, t * P : (t + 1) * P].bitcast(FP8X4)
 
-        banks = new_banks("acc_a")
-        for h in range(2):
-            first_stage_pass(banks, h, e4m3_columns(w1_q[0][0]), w1_q[0][1], g_a0[h], s_a, True, False)
-        for h in range(2):
-            picked = gather_words(tab_a1, l_a, h, "g_a1%d" % h)
-            first_stage_pass(banks, h, e4m3_columns(w1_q[1][0]), w1_q[1][1], picked, s_a1, False, True)
-        ws = keep.tile([P, 4 * H], U8, name="ws", align_bytes=64)
+        def e2m1_columns(a):
+            return lambda t: w2[:, (a * H + t * P) * 2 : (a * H + (t + 1) * P) * 2].bitcast(FP4X4)
 
-        def deal_scales(first, passes):
-            cols = slice(first * H, (first + passes) * H)
-            nc.vector.tensor_copy(
-                ws[:, cols].rearrange("p (a t m) -> p a t m", a=passes, t=PACK),
-                ws_raw[:, cols].rearrange("p (a m t) -> p a t m", a=passes, t=PACK),
-            )
-
-        deal_scales(0, 3)
-        res_a = new_results("a")
-        for t, h in EMPTY_ORDER:
-            empty_bank(nc.scalar.copy, res_a, banks, t, h)
-        aj = keep.tile([P, PACK, J], F32, name="aj")
-        for t in range(PACK):
+        def pick_a(t):
             nc.vector.tensor_copy(aj[:, t, :], res_a[t][:].indirect(p_a[:]))
 
-        banks = new_banks("acc_d")
-        g_d = [gather_words(tab_d, l_d, h, "g_d%d" % h) for h in range(2)]
-        w3_q = quantize(weave_dealt(nc.scalar.copy, w3_raw, "w3_woven"), H, "w3")
-        for h in range(2):
-            first_stage_pass(banks, h, e4m3_columns(w3_q[0]), w3_q[1], g_d[h], s_d, True, True)
-        deal_scales(3, 1)
-        res_d = new_results("d")
+        def pick_d(t):
+            nc.vector.tensor_tensor(da[:, t, :], res_d[t][:].indirect(p_d[:]), aj[:, t, :], ALU.subtract)
+
+        g_a0 = gather_words(tab_a0, l_a, 0, S, "g_a0", "g_a0", 1)
+        s_a = gather_scales(win_a, l_a, "s_a")
+        s_d = gather_scales(win_d, l_d, "s_d")
+        w1_q = [quantize(weave_dealt(w1_raw[0], "w1_woven0"), H, "w1_0")]
+        s_b = gather_scales(win_b, l_b, "s_b")
+        tab_b = [load_table_pass(tab2_words, 0, "tab_b0")]
+        move_up(s_b1, s_b, 4)
+        move_up(s_b2, s_b, 8)
+        w1_q.append(quantize(weave_dealt(w1_raw[1], "w1_woven1"), H, "w1_1"))
+        banks = new_banks("acc_a")
+        first_stage_pass(banks, e4m3_columns(w1_q[0][0]), w1_q[0][1], halves(g_a0), s_a[4:P, :], True, False)
+        g_a1 = [gather_words(tab_a1, l_a, h * HALF, HALF, "g_a1%d" % h, "woven", 2)[:] for h in range(2)]
+        first_stage_pass(banks, e4m3_columns(w1_q[1][0]), w1_q[1][1], g_a1, s_a[8:P, :], False, True)
+        tab_b.append(load_table_pass(tab2_words, 1, "tab_b1"))
+        ws = ring.tile([P, 4 * H], U8, tag="woven", bufs=2, name="ws", align_bytes=64)
+        nc.vector.tensor_copy(
+            ws[:].rearrange("p (a t m) -> p a t m", a=4, t=PACK), ws_raw[:].rearrange("p (a m t) -> p a t m", a=4, t=PACK)
+        )
+        res_a = new_results("a", "ab")
         for t, h in EMPTY_ORDER:
-            empty_bank(nc.scalar.copy, res_d, banks, t, h)
-        w2 = keep.tile([P, 3 * 2 * H], U8, name="w2", align_bytes=64)
+            empty_bank(res_a, banks, t, h)
+        aj = keep.tile([P, PACK, J], F32, name="aj")
+        for t in range(PACK):
+            pick_a(t)
+
+        w3_woven = weave_dealt(w3_raw, "w3_woven")
+        g_d = [gather_words(tab_d, l_d, 0, HALF, "g_d0", "ab2", 1)[:]]
+        w3_q = quantize(w3_woven, H, "w3")
+        g_d.append(gather_words(tab_d, l_d, HALF, HALF, "g_d1", "ab3", 1)[:])
+        banks = new_banks("acc_d")
+        first_stage_pass(banks, e4m3_columns(w3_q[0]), w3_q[1], g_d, s_d[12:P, :], True, True)
+        tab_b.append(load_table_pass(tab2_words, 2, "tab_b2"))
+        w2 = ring.tile([P, 3 * 2 * H], U8, tag="woven", bufs=2, name="w2", align_bytes=64)
         nc.scalar.copy(
             w2[:].bitcast(U16).rearrange("p (a t m) -> p a t m", a=3, t=PACK),
             w2_raw[:].bitcast(U16).rearrange("p a (m t) -> p a t m", t=PACK),
         )
+        res_d = new_results("d", "dh")
+        for t, h in EMPTY_ORDER:
+            empty_bank(res_d, banks, t, h)
 
-        def e2m1_columns(a):
-            return lambda t: w2[:, (a * H + t * P) * 2 : (a * H + (t + 1) * P) * 2].bitcast(FP4X4)
-
-        s_b_planes = [s_b, s_b1, s_b2]
         da = keep.tile([P, PACK, J], F32, name="da")
         banks = new_banks("acc_b")
-        for a in range(3):
-            for h in range(2):
-                picked = gather_words(tab_b[a], l_b, h, "g_b%d%d" % (a, h))
-                first_stage_pass(
-                    banks, h, e2m1_columns(a), ws[:, a * H : (a + 1) * H], picked, s_b_planes[a], a == 0, a == 2
-                )
-            if a < 2:
-                for t in (2 * a, 2 * a + 1):
-                    nc.vector.tensor_tensor(da[:, t, :], res_d[t][:].indirect(p_d[:]), aj[:, t, :], ALU.subtract)
-        res_b = new_results("b")
+
+        def b_pass(a, picked, plane):
+            first_stage_pass(banks, e2m1_columns(a), ws[:, a * H : (a + 1) * H], picked, plane, a == 0, a == 2)
+
+        g_b0 = gather_words(tab_b[0], l_b, 0, S, "g_b0", "ab2", 1)
+        b_pass(0, halves(g_b0), s_b)
+        w4_raw = ring.tile([P, H], I32, tag="table", bufs=3, name="w4_raw")
+        nc.sync.dma_start(w4_raw[:], w4_words[0].rearrange("p c i -> p (c i)").bitcast(I32))
+        pick_d(0)
+        pick_d(1)
+        g_b1 = gather_words(tab_b[1], l_b, 0, S, "g_b1", "dh1", 1)
+        b_pass(1, halves(g_b1), s_b1)
+        w5_raw = ring.tile([P, PACK, N_OUT], F32, tag="table", bufs=3, name="w5_raw")
+        nc.sync.dma_start(w5_raw[:], w5.rearrange("(p j) c -> p j c", j=PACK))
+        pick_d(2)
+        g_b2 = [gather_words(tab_b[2], l_b, h * HALF, HALF, "g_b2%d" % h, ("dh2", "dh0")[h], 1)[:] for h in range(2)]
+        b_pass(2, g_b2, s_b2)
+        pick_d(3)
+        res_b = new_results("b", "ab")
         for t, h in EMPTY_ORDER:
-            empty_bank(nc.vector.tensor_copy if (h == 0 and t >= 2) else nc.scalar.copy, res_b, banks, t, h)
+            empty_bank(res_b, banks, t, h)
         w4 = keep.tile([P, H], U32, name="w4", align_bytes=64)
         nc.scalar.copy(
             w4[:].rearrange("p (t m) -> p m t", t=PACK), w4_raw[:].bitcast(U32).rearrange("p (m t) -> p m t", t=PACK)
@@ -252,24 +246,20 @@ def tile_list_cell_sharing_scores_kernel(
 
         z = keep.tile([P, PACK, J], F32, name="z")
 
-        def join(first, width):
-            cols = slice(first, first + width)
+        def difference(piece, t, tag):
+            first, width = piece
+            ba = ring.tile([P, width], F32, tag=tag, bufs=1, name="ba%d_%d" % (first, t), align_bytes=64)
             offsets = p_b[:, first // 16 : (first + width) // 16]
-            diffs = []
+            nc.vector.tensor_tensor(ba[:], res_b[t][:].indirect(offsets), aj[:, t, first : first + width], ALU.subtract)
+            return ba
 
-            def product(t):
-                nc.vector.scalar_tensor_tensor(
-                    z[:, t, cols], diffs[t][:], gain_t[:, t : t + 1], da[:, t, cols], ALU.mult, ALU.mult
-                )
+        def product(piece, t, ba):
+            cols = slice(piece[0], piece[0] + piece[1])
+            nc.vector.scalar_tensor_tensor(z[:, t, cols], ba[:], gain_t[:, t : t + 1], da[:, t, cols], ALU.mult, ALU.mult)
 
-            for t in range(PACK):
-                ba = ring.tile([P, width], F32, tag="ba", bufs=3, name="ba%d_%d" % (first, t))
-                nc.vector.tensor_tensor(ba[:], res_b[t][:].indirect(offsets), aj[:, t, cols], ALU.subtract)
-                diffs.append(ba)
-                if t > 0:
-                    product(t - 1)
-            product(PACK - 1)
-            return weave(nc.scalar.copy, z[:, :, cols], width, "z_woven%d" % first)
+        def weave_z(piece):
+            first, width = piece
+            return weave(nc.scalar.copy, z[:, :, first : first + width], width, "z_woven%d" % first, "z_woven%d" % first)
 
         def hidden(first, width, z_woven):
             cols = slice(first, first + width)
@@ -291,14 +281,14 @@ def tile_list_cell_sharing_scores_kernel(
 
         def larger(first, width, ys, mover):
             cols = slice(first, first + width)
-            hid = ring.tile([P, PACK, width], F32, tag="result", bufs=8, name="h%d" % first)
+            hid = ring.tile([P, PACK, width], F32, tag="dh1" if first else "dh2", bufs=1, name="h%d" % first, align_bytes=64)
             for t in range(PACK):
                 nc.vector.scalar_tensor_tensor(hid[:, t, :], ys[t][:], b4_t[:, t : t + 1], z[:, t, cols], ALU.add, ALU.max)
-            return weave(mover, hid[:], width, "h_woven%d" % first)
+            return weave(mover, hid[:], width, "h_woven%d" % first, "h_woven%d" % first)
 
         def scores(first, width, h_woven, w5_q, last):
             codes, scales = quantize(h_woven, width, "h%d" % first)
-            staged = ring.tile([P, N_OUT // P, width], F32, tag="result", bufs=8, name="staged%d" % first)
+            staged = ring.tile([P, N_OUT // P, width], F32, tag="dh3" if first else "dh0", bufs=1, name="staged%d" % first, align_bytes=64)
             for n in range(N_OUT // P):
                 acc = psum.tile([P, width], F32, tag="bank", name="o%d_%d" % (first, n))
                 nc.tensor.matmul_mx(
@@ -312,15 +302,32 @@ def tile_list_cell_sharing_scores_kernel(
                 )
                 mover = nc.vector.tensor_copy if (last and n == 1) else nc.scalar.copy
                 mover(staged[:, n, :], acc[:])
-            nc.sync.dma_start(out.rearrange("(n p) j -> p n j", p=P)[:, :, first : first + width], staged[:])
+                nc.sync.dma_start(out[n * P : (n + 1) * P, first : first + width], staged[:, n, :])
 
-        z0 = join(*PIECES[0])
+        one, two = PIECES
+        ba0 = difference(one, 0, "ba_even")
+        ba1 = difference(one, 1, "ba_odd")
+        product(one, 0, ba0)
+        early = difference(two, 0, "ba_early")
+        product(one, 1, ba1)
+        ba2 = difference(one, 2, "ba_even")
+        product(two, 0, early)
+        ba3 = difference(one, 3, "ba_odd")
+        product(one, 2, ba2)
+        product(one, 3, ba3)
+        z0 = weave_z(one)
         w5_woven = keep.tile([P, PACK * N_OUT], BF16, name="w5_woven", align_bytes=64)
         nc.scalar.copy(
             w5_woven[:].rearrange("p (c i t) -> p c t i", t=PACK, i=4), w5_raw[:].rearrange("p t (c i) -> p c t i", i=4)
         )
+        ba1 = difference(two, 1, "ba_odd")
+        ba3 = difference(two, 3, "ba_even")
+        product(two, 1, ba1)
         y0 = hidden(*PIECES[0], z0)
-        z1 = join(*PIECES[1])
+        ba2 = difference(two, 2, "z_woven0")
+        product(two, 3, ba3)
+        product(two, 2, ba2)
+        z1 = weave_z(two)
         h0 = larger(*PIECES[0], y0, nc.scalar.copy)
         w5_q = quantize(w5_woven, N_OUT, "w5")
         y1 = hidden(*PIECES[1], z1)

@@ -2,7 +2,11 @@ from contextlib import ExitStack
 
 import concourse.mybir as mybir
 
-T, S, H, J, N_OUT = 4096, 1024, 512, 512, 384
+T = 4096
+S = 1024
+H = 512
+J = 512
+N_OUT = 384
 FLOPS = 2 * H * S * (1024 + 1536 + 512) + 2 * H * H * J + 2 * H * N_OUT * J
 
 F32 = mybir.dt.float32
@@ -17,8 +21,11 @@ ALU = mybir.AluOpType
 
 P = 128
 PACK = 4
+K_PASS = P * PACK
 HALF = 512
+MOVED_ROWS = 112
 PIECES = ((0, 256), (256, 256))
+BANK_ORDER = ((0, 0), (1, 0), (0, 1), (1, 1), (2, 0), (2, 1), (3, 0), (3, 1))
 
 
 def tile_list_cell_sharing_scores_kernel(
@@ -41,24 +48,30 @@ def tile_list_cell_sharing_scores_kernel(
             engine.memset(plane[:].bitcast(I32), 0)
             return plane
 
-        def load_packed_scales(queue, window, first, scales):
+        def load_packed_scales(window, first, scales):
             rows = 4 * scales.shape[0]
             for q in range(4):
-                queue.dma_start(
+                nc.sync.dma_start(
                     window[32 * q + first : 32 * q + first + rows, :].bitcast(I32),
                     scales[:, 4 * q : 4 * q + 4, :].bitcast(I32),
                 )
 
-        def load_scales_side_by_side(queue, planes, first, scales):
+        def load_scales_side_by_side(planes, first, scales):
             passes = scales.shape[0]
             for r in range(4):
-                queue.dma_start(
+                nc.sync.dma_start(
                     planes[first + r : P : 32].bitcast(I32).rearrange("q (a c) -> q a c", a=passes),
                     scales[:, r:16:4, :].bitcast(I32).rearrange("a q c -> q a c"),
                 )
 
+        def load_two_passes_scales(window, scales):
+            for r in range(4):
+                nc.sync.dma_start(
+                    window[r:P:16, :].bitcast(I32), scales[:, r:16:4, :].bitcast(I32).rearrange("a q t -> q a t")
+                )
+
         def move_up(plane, picked, first):
-            nc.sync.dma_start(plane[0:112, :].bitcast(I32), picked[first : first + 112, :].bitcast(I32))
+            nc.sync.dma_start(plane[0:MOVED_ROWS, :].bitcast(I32), picked[first : first + MOVED_ROWS, :].bitcast(I32))
 
         def load_table_pass(words, a, name):
             window = ring.tile([P, T], I32, tag="table", bufs=3, name=name)
@@ -91,11 +104,11 @@ def tile_list_cell_sharing_scores_kernel(
             )
             return woven
 
-        def weave(mover, planes, width, name, tag):
-            woven = ring.tile([P, PACK * width], BF16, tag=tag, bufs=1, name=name, align_bytes=64)
+        def weave(mover, slices, width, name):
+            woven = ring.tile([P, PACK * width], BF16, tag=name, bufs=1, name=name, align_bytes=64)
             mover(
                 woven[:].rearrange("p (c i t) -> p c t i", t=PACK, i=4),
-                planes.rearrange("p t (c i) -> p c t i", i=4),
+                slices.rearrange("p t (c i) -> p c t i", i=4),
             )
             return woven
 
@@ -106,13 +119,19 @@ def tile_list_cell_sharing_scores_kernel(
             return codes, scales
 
         def new_banks(name):
-            return [[psum.tile([P, HALF], F32, tag="bank", name="%s%d%d" % (name, t, h)) for h in range(2)] for t in range(PACK)]
+            return [
+                [psum.tile([P, HALF], F32, tag="bank", name="%s%d%d" % (name, t, half)) for half in range(2)]
+                for t in range(PACK)
+            ]
 
         def new_results(name, tag):
-            return [ring.tile([P, S], F32, tag="%s%d" % (tag, t), bufs=1, name="%s%d" % (name, t), align_bytes=64) for t in range(PACK)]
+            return [
+                ring.tile([P, S], F32, tag="%s%d" % (tag, t), bufs=1, name="%s%d" % (name, t), align_bytes=64)
+                for t in range(PACK)
+            ]
 
         def first_stage_pass(banks, lhs, lhs_scales, picked, picked_scales, start, stop):
-            for t, half in EMPTY_ORDER:
+            for t, half in BANK_ORDER:
                 nc.tensor.matmul_mx(
                     out=banks[t][half][:],
                     lhsT=lhs(t),
@@ -126,20 +145,16 @@ def tile_list_cell_sharing_scores_kernel(
         def halves(picked):
             return [picked[:, 0:HALF], picked[:, HALF:S]]
 
-        def empty_bank(results, banks, t, half):
-            nc.scalar.copy(results[t][:, half * HALF : (half + 1) * HALF], banks[t][half][:])
-
-        EMPTY_ORDER = ((0, 0), (1, 0), (0, 1), (1, 1), (2, 0), (2, 1), (3, 0), (3, 1))
+        def empty_banks(results, banks):
+            for t, half in BANK_ORDER:
+                nc.scalar.copy(results[t][:, half * HALF : (half + 1) * HALF], banks[t][half][:])
 
         win_a = zeroed_bytes(nc.vector, T, "win_a")
-        win_d = zeroed_bytes(nc.vector, T, "win_d")
+        win_d = zeroed_bytes(nc.gpsimd, T, "win_d")
         win_b = zeroed_bytes(nc.vector, T, "win_b")
-        ws_raw = zeroed_bytes(nc.vector, 4 * H, "ws_raw")
+        ws_raw = zeroed_bytes(nc.gpsimd, 4 * H, "ws_raw")
         s_b1 = zeroed_bytes(nc.vector, S, "s_b1")
         s_b2 = zeroed_bytes(nc.vector, S, "s_b2")
-
-        load_scales_side_by_side(nc.gpsimd, win_d[:], 12, tab3_scales)
-        load_packed_scales(nc.gpsimd, win_b, 0, tab2_scales)
 
         l_a = load_list(offs, "l_a")
         l_d = load_list(offs3, "l_d")
@@ -149,17 +164,20 @@ def tile_list_cell_sharing_scores_kernel(
         p_b = load_list(pos2, "p_b")
         gain_t = keep.tile([P, PACK], F32, name="gain_t")
         nc.sync.dma_start(gain_t[:], gain.rearrange("(p t) -> p t", t=PACK))
-        tab_a0 = load_table_pass(tab_words, 0, "tab_a0")
-        load_packed_scales(nc.sync, win_a, 4, tab_scales)
-        w1_raw = [load_rows(w1[0:512, :], "w1_raw0")]
-        w1_raw.append(load_rows(w1[512:1024, :], "w1_raw1"))
-        tab_a1 = load_table_pass(tab_words, 1, "tab_a1")
-        load_scales_side_by_side(nc.sync, ws_raw[:, 0 : 3 * H], 0, w2_scales)
-        w3_raw = load_rows(w3, "w3_raw")
-        load_scales_side_by_side(nc.sync, ws_raw[:, 3 * H : 4 * H], 0, w4_scales)
-        tab_d = load_table_pass(tab3_words, 0, "tab_d")
+        w1_raw = [load_rows(w1[0:K_PASS, :], "w1_raw0")]
+        load_packed_scales(win_a, 4, tab_scales)
+        load_scales_side_by_side(win_d[:], 12, tab3_scales)
+        load_two_passes_scales(win_b, tab2_scales[0:2])
+        load_scales_side_by_side(win_b[:], 8, tab2_scales[2:3])
+        load_scales_side_by_side(ws_raw[:, 0 : 3 * H], 0, w2_scales)
+        load_scales_side_by_side(ws_raw[:, 3 * H : 4 * H], 0, w4_scales)
         b4_t = keep.tile([P, PACK], F32, name="b4_t")
         nc.sync.dma_start(b4_t[:], b4.rearrange("(p t) -> p t", t=PACK))
+        tab_a0 = load_table_pass(tab_words, 0, "tab_a0")
+        w1_raw.append(load_rows(w1[K_PASS : 2 * K_PASS, :], "w1_raw1"))
+        tab_a1 = load_table_pass(tab_words, 1, "tab_a1")
+        w3_raw = load_rows(w3, "w3_raw")
+        tab_d = load_table_pass(tab3_words, 0, "tab_d")
         w2_raw = keep.tile([P, 3, 2 * H], U8, name="w2_raw")
         nc.sync.dma_start(w2_raw[:].bitcast(I32), w2_words.bitcast(I32).rearrange("a p c -> p a c"))
 
@@ -175,35 +193,35 @@ def tile_list_cell_sharing_scores_kernel(
         def pick_d(t):
             nc.vector.tensor_tensor(da[:, t, :], res_d[t][:].indirect(p_d[:]), aj[:, t, :], ALU.subtract)
 
-        g_a0 = gather_words(tab_a0, l_a, 0, S, "g_a0", "g_a0", 1)
         s_a = gather_scales(win_a, l_a, "s_a")
         s_d = gather_scales(win_d, l_d, "s_d")
         w1_q = [quantize(weave_dealt(w1_raw[0], "w1_woven0"), H, "w1_0")]
         s_b = gather_scales(win_b, l_b, "s_b")
-        tab_b = [load_table_pass(tab2_words, 0, "tab_b0")]
-        move_up(s_b1, s_b, 4)
-        move_up(s_b2, s_b, 8)
-        w1_q.append(quantize(weave_dealt(w1_raw[1], "w1_woven1"), H, "w1_1"))
-        banks = new_banks("acc_a")
-        first_stage_pass(banks, e4m3_columns(w1_q[0][0]), w1_q[0][1], halves(g_a0), s_a[4:P, :], True, False)
-        g_a1 = [gather_words(tab_a1, l_a, h * HALF, HALF, "g_a1%d" % h, "woven", 2)[:] for h in range(2)]
-        first_stage_pass(banks, e4m3_columns(w1_q[1][0]), w1_q[1][1], g_a1, s_a[8:P, :], False, True)
-        tab_b.append(load_table_pass(tab2_words, 1, "tab_b1"))
-        ws = ring.tile([P, 4 * H], U8, tag="woven", bufs=2, name="ws", align_bytes=64)
+        ws = keep.tile([P, 4 * H], U8, name="ws", align_bytes=64)
         nc.vector.tensor_copy(
             ws[:].rearrange("p (a t m) -> p a t m", a=4, t=PACK), ws_raw[:].rearrange("p (a m t) -> p a t m", a=4, t=PACK)
         )
+        g_a0 = gather_words(tab_a0, l_a, 0, S, "g_a0", "g_a0", 1)
+        move_up(s_b1, s_b, 16)
+        move_up(s_b2, s_b, 8)
+        tab_b = [load_table_pass(tab2_words, 0, "tab_b0")]
+        w1_q.append(quantize(weave_dealt(w1_raw[1], "w1_woven1"), H, "w1_1"))
+        banks = new_banks("acc_a")
+        first_stage_pass(banks, e4m3_columns(w1_q[0][0]), w1_q[0][1], halves(g_a0), s_a[4:P, :], True, False)
+        g_a1 = [gather_words(tab_a1, l_a, n * HALF, HALF, "g_a1%d" % n, "woven", 2)[:] for n in range(2)]
+        first_stage_pass(banks, e4m3_columns(w1_q[1][0]), w1_q[1][1], g_a1, s_a[8:P, :], False, True)
+        tab_b.append(load_table_pass(tab2_words, 1, "tab_b1"))
         res_a = new_results("a", "ab")
-        for t, h in EMPTY_ORDER:
-            empty_bank(res_a, banks, t, h)
+        empty_banks(res_a, banks)
         aj = keep.tile([P, PACK, J], F32, name="aj")
-        for t in range(PACK):
+        for t in range(PACK - 1):
             pick_a(t)
 
         w3_woven = weave_dealt(w3_raw, "w3_woven")
         g_d = [gather_words(tab_d, l_d, 0, HALF, "g_d0", "ab2", 1)[:]]
         w3_q = quantize(w3_woven, H, "w3")
-        g_d.append(gather_words(tab_d, l_d, HALF, HALF, "g_d1", "ab3", 1)[:])
+        g_d.append(gather_words(tab_d, l_d, HALF, HALF, "g_d1", "ab1", 1)[:])
+        pick_a(PACK - 1)
         banks = new_banks("acc_d")
         first_stage_pass(banks, e4m3_columns(w3_q[0]), w3_q[1], g_d, s_d[12:P, :], True, True)
         tab_b.append(load_table_pass(tab2_words, 2, "tab_b2"))
@@ -213,8 +231,7 @@ def tile_list_cell_sharing_scores_kernel(
             w2_raw[:].bitcast(U16).rearrange("p a (m t) -> p a t m", t=PACK),
         )
         res_d = new_results("d", "dh")
-        for t, h in EMPTY_ORDER:
-            empty_bank(res_d, banks, t, h)
+        empty_banks(res_d, banks)
 
         da = keep.tile([P, PACK, J], F32, name="da")
         banks = new_banks("acc_b")
@@ -222,23 +239,22 @@ def tile_list_cell_sharing_scores_kernel(
         def b_pass(a, picked, plane):
             first_stage_pass(banks, e2m1_columns(a), ws[:, a * H : (a + 1) * H], picked, plane, a == 0, a == 2)
 
-        g_b0 = gather_words(tab_b[0], l_b, 0, S, "g_b0", "ab2", 1)
+        pick_d(0)
+        g_b0 = gather_words(tab_b[0], l_b, 0, S, "g_b0", "dh0", 1)
         b_pass(0, halves(g_b0), s_b)
         w4_raw = ring.tile([P, H], I32, tag="table", bufs=3, name="w4_raw")
         nc.sync.dma_start(w4_raw[:], w4_words[0].rearrange("p c i -> p (c i)").bitcast(I32))
-        pick_d(0)
         pick_d(1)
         g_b1 = gather_words(tab_b[1], l_b, 0, S, "g_b1", "dh1", 1)
         b_pass(1, halves(g_b1), s_b1)
         w5_raw = ring.tile([P, PACK, N_OUT], F32, tag="table", bufs=3, name="w5_raw")
         nc.sync.dma_start(w5_raw[:], w5.rearrange("(p j) c -> p j c", j=PACK))
         pick_d(2)
-        g_b2 = [gather_words(tab_b[2], l_b, h * HALF, HALF, "g_b2%d" % h, ("dh2", "dh0")[h], 1)[:] for h in range(2)]
+        g_b2 = [gather_words(tab_b[2], l_b, n * HALF, HALF, "g_b2%d" % n, ("dh2", "dh0")[n], 1)[:] for n in range(2)]
         b_pass(2, g_b2, s_b2)
         pick_d(3)
         res_b = new_results("b", "ab")
-        for t, h in EMPTY_ORDER:
-            empty_bank(res_b, banks, t, h)
+        empty_banks(res_b, banks)
         w4 = keep.tile([P, H], U32, name="w4", align_bytes=64)
         nc.scalar.copy(
             w4[:].rearrange("p (t m) -> p m t", t=PACK), w4_raw[:].bitcast(U32).rearrange("p (m t) -> p m t", t=PACK)
@@ -259,10 +275,10 @@ def tile_list_cell_sharing_scores_kernel(
 
         def weave_z(piece):
             first, width = piece
-            return weave(nc.scalar.copy, z[:, :, first : first + width], width, "z_woven%d" % first, "z_woven%d" % first)
+            return weave(nc.scalar.copy, z[:, :, first : first + width], width, "z_woven%d" % first)
 
-        def hidden(first, width, z_woven):
-            cols = slice(first, first + width)
+        def hidden(piece, z_woven):
+            first, width = piece
             codes, scales = quantize(z_woven, width, "z%d" % first)
             ys = []
             for t in range(PACK):
@@ -279,16 +295,18 @@ def tile_list_cell_sharing_scores_kernel(
                 ys.append(y)
             return ys
 
-        def larger(first, width, ys, mover):
+        def larger(piece, ys, mover, tag):
+            first, width = piece
             cols = slice(first, first + width)
-            hid = ring.tile([P, PACK, width], F32, tag="dh1" if first else "dh2", bufs=1, name="h%d" % first, align_bytes=64)
+            hid = ring.tile([P, PACK, width], F32, tag=tag, bufs=1, name="h%d" % first, align_bytes=64)
             for t in range(PACK):
                 nc.vector.scalar_tensor_tensor(hid[:, t, :], ys[t][:], b4_t[:, t : t + 1], z[:, t, cols], ALU.add, ALU.max)
-            return weave(mover, hid[:], width, "h_woven%d" % first, "h_woven%d" % first)
+            return weave(mover, hid[:], width, "h_woven%d" % first)
 
-        def scores(first, width, h_woven, w5_q, last):
+        def scores(piece, h_woven, movers, tag):
+            first, width = piece
             codes, scales = quantize(h_woven, width, "h%d" % first)
-            staged = ring.tile([P, N_OUT // P, width], F32, tag="dh3" if first else "dh0", bufs=1, name="staged%d" % first, align_bytes=64)
+            staged = ring.tile([P, N_OUT // P, width], F32, tag=tag, bufs=1, name="staged%d" % first, align_bytes=64)
             for n in range(N_OUT // P):
                 acc = psum.tile([P, width], F32, tag="bank", name="o%d_%d" % (first, n))
                 nc.tensor.matmul_mx(
@@ -300,8 +318,7 @@ def tile_list_cell_sharing_scores_kernel(
                     start=True,
                     stop=True,
                 )
-                mover = nc.vector.tensor_copy if (last and n == 1) else nc.scalar.copy
-                mover(staged[:, n, :], acc[:])
+                movers[n](staged[:, n, :], acc[:])
                 nc.sync.dma_start(out[n * P : (n + 1) * P, first : first + width], staged[:, n, :])
 
         one, two = PIECES
@@ -323,14 +340,14 @@ def tile_list_cell_sharing_scores_kernel(
         ba1 = difference(two, 1, "ba_odd")
         ba3 = difference(two, 3, "ba_even")
         product(two, 1, ba1)
-        y0 = hidden(*PIECES[0], z0)
+        y0 = hidden(one, z0)
         ba2 = difference(two, 2, "z_woven0")
         product(two, 3, ba3)
         product(two, 2, ba2)
         z1 = weave_z(two)
-        h0 = larger(*PIECES[0], y0, nc.scalar.copy)
+        h0 = larger(one, y0, nc.scalar.copy, "dh2")
         w5_q = quantize(w5_woven, N_OUT, "w5")
-        y1 = hidden(*PIECES[1], z1)
-        scores(*PIECES[0], h0, w5_q, False)
-        h1 = larger(*PIECES[1], y1, nc.vector.tensor_copy)
-        scores(*PIECES[1], h1, w5_q, True)
+        y1 = hidden(two, z1)
+        scores(one, h0, [nc.scalar.copy] * 3, "dh0")
+        h1 = larger(two, y1, nc.vector.tensor_copy, "dh1")
+        scores(two, h1, [nc.scalar.copy, nc.vector.tensor_copy, nc.scalar.copy], "dh3")

from contextlib import ExitStack

import concourse.mybir as mybir

T = 4096
S = 1024
H = 512
J = 512
N_OUT = 384
FLOPS = 2 * H * S * (1024 + 1536 + 512) + 2 * H * H * J + 2 * H * N_OUT * J

F32 = mybir.dt.float32
BF16 = mybir.dt.bfloat16
I32 = mybir.dt.int32
U32 = mybir.dt.uint32
U16 = mybir.dt.uint16
U8 = mybir.dt.uint8
FP8X4 = mybir.dt.float8_e4m3fn_x4
FP4X4 = mybir.dt.float4_e2m1fn_x4
ALU = mybir.AluOpType

P = 128
PACK = 4
K_PASS = P * PACK
HALF = 512
MOVED_ROWS = 112
PIECES = ((0, 256), (256, 256))
BANK_ORDER = ((0, 0), (1, 0), (0, 1), (1, 1), (2, 0), (2, 1), (3, 0), (3, 1))


def tile_list_cell_sharing_scores_kernel(
    tc, tab_words, tab_scales, tab2_words, tab2_scales, tab3_words, tab3_scales, offs, offs2, offs3,
    pos1, pos2, pos3, w1, w2_words, w2_scales, w3, gain, w4_words, w4_scales, b4, w5, out,
):
    nc = tc.nc
    with ExitStack() as ctx:
        keep = ctx.enter_context(tc.tile_pool(name="keep", bufs=1))
        ring = ctx.enter_context(tc.tile_pool(name="ring", bufs=1))
        psum = ctx.enter_context(tc.psum_pool(name="psum", bufs=8))

        def load_list(src, name):
            lst = keep.tile([P, src.shape[1]], U16, name=name)
            nc.sync.dma_start(lst[:], src)
            return lst

        def zeroed_bytes(engine, width, name):
            plane = keep.tile([P, width], U8, name=name, align_bytes=64)
            engine.memset(plane[:].bitcast(I32), 0)
            return plane

        def load_packed_scales(window, first, scales):
            rows = 4 * scales.shape[0]
            for q in range(4):
                nc.sync.dma_start(
                    window[32 * q + first : 32 * q + first + rows, :].bitcast(I32),
                    scales[:, 4 * q : 4 * q + 4, :].bitcast(I32),
                )

        def load_scales_side_by_side(planes, first, scales):
            passes = scales.shape[0]
            for r in range(4):
                nc.sync.dma_start(
                    planes[first + r : P : 32].bitcast(I32).rearrange("q (a c) -> q a c", a=passes),
                    scales[:, r:16:4, :].bitcast(I32).rearrange("a q c -> q a c"),
                )

        def load_two_passes_scales(window, scales):
            for r in range(4):
                nc.sync.dma_start(
                    window[r:P:16, :].bitcast(I32), scales[:, r:16:4, :].bitcast(I32).rearrange("a q t -> q a t")
                )

        def move_up(plane, picked, first):
            nc.sync.dma_start(plane[0:MOVED_ROWS, :].bitcast(I32), picked[first : first + MOVED_ROWS, :].bitcast(I32))

        def load_table_pass(words, a, name):
            window = ring.tile([P, T], I32, tag="table", bufs=3, name=name)
            nc.sync.dma_start(window[:], words[a].rearrange("p t i -> p (t i)").bitcast(I32))
            return window

        def load_rows(rows, name):
            width = rows.shape[1]
            raw = ring.tile([P, PACK, width], F32, tag="raw", bufs=3, name=name)
            nc.sync.dma_start(raw[:], rows.rearrange("(p j) c -> p j c", j=PACK))
            return raw

        def gather_scales(window, lst, name):
            picked = keep.tile([P, S], U8, name=name, align_bytes=64)
            nc.vector.tensor_copy(picked[:], window[:].indirect(lst[:]))
            return picked

        def gather_words(window, lst, first, count, name, tag, bufs):
            picked = ring.tile([P, count], U32, tag=tag, bufs=bufs, name=name, align_bytes=64)
            nc.vector.tensor_copy(
                picked[:], window[:].bitcast(U32).indirect(lst[:, first // 16 : (first + count) // 16])
            )
            return picked

        def weave_dealt(raw, name):
            woven = ring.tile([P, PACK * H], BF16, tag="woven", bufs=2, name=name, align_bytes=64)
            nc.scalar.copy(
                woven[:].rearrange("p (u e m j) -> p u m j e", u=2, e=2, j=PACK),
                raw[:].rearrange("p j (m u e) -> p u m j e", u=2, e=2),
            )
            return woven

        def weave(mover, slices, width, name):
            woven = ring.tile([P, PACK * width], BF16, tag=name, bufs=1, name=name, align_bytes=64)
            mover(
                woven[:].rearrange("p (c i t) -> p c t i", t=PACK, i=4),
                slices.rearrange("p t (c i) -> p c t i", i=4),
            )
            return woven

        def quantize(woven, width, name):
            codes = keep.tile([P, width], U32, name=name + "_codes", align_bytes=64)
            scales = keep.tile([P, width], U8, name=name + "_scales", align_bytes=64)
            nc.vector.quantize_mx(out=codes[:].bitcast(FP8X4), scales=scales[:], in_=woven[:])
            return codes, scales

        def new_banks(name):
            return [
                [psum.tile([P, HALF], F32, tag="bank", name="%s%d%d" % (name, t, half)) for half in range(2)]
                for t in range(PACK)
            ]

        def new_results(name, tag):
            return [
                ring.tile([P, S], F32, tag="%s%d" % (tag, t), bufs=1, name="%s%d" % (name, t), align_bytes=64)
                for t in range(PACK)
            ]

        def first_stage_pass(banks, lhs, lhs_scales, picked, picked_scales, start, stop):
            for t, half in BANK_ORDER:
                nc.tensor.matmul_mx(
                    out=banks[t][half][:],
                    lhsT=lhs(t),
                    lhsT_scale=lhs_scales[:, t * P : (t + 1) * P],
                    rhs=picked[half].bitcast(FP8X4),
                    rhs_scale=picked_scales[:, half * HALF : (half + 1) * HALF],
                    start=start,
                    stop=stop,
                )

        def halves(picked):
            return [picked[:, 0:HALF], picked[:, HALF:S]]

        def empty_banks(results, banks):
            for t, half in BANK_ORDER:
                nc.scalar.copy(results[t][:, half * HALF : (half + 1) * HALF], banks[t][half][:])

        win_a = zeroed_bytes(nc.vector, T, "win_a")
        win_d = zeroed_bytes(nc.gpsimd, T, "win_d")
        win_b = zeroed_bytes(nc.vector, T, "win_b")
        ws_raw = zeroed_bytes(nc.gpsimd, 4 * H, "ws_raw")
        s_b1 = zeroed_bytes(nc.vector, S, "s_b1")
        s_b2 = zeroed_bytes(nc.vector, S, "s_b2")

        l_a = load_list(offs, "l_a")
        l_d = load_list(offs3, "l_d")
        l_b = load_list(offs2, "l_b")
        p_a = load_list(pos1, "p_a")
        p_d = load_list(pos3, "p_d")
        p_b = load_list(pos2, "p_b")
        gain_t = keep.tile([P, PACK], F32, name="gain_t")
        nc.sync.dma_start(gain_t[:], gain.rearrange("(p t) -> p t", t=PACK))
        w1_raw = [load_rows(w1[0:K_PASS, :], "w1_raw0")]
        load_packed_scales(win_a, 4, tab_scales)
        load_scales_side_by_side(win_d[:], 12, tab3_scales)
        load_two_passes_scales(win_b, tab2_scales[0:2])
        load_scales_side_by_side(win_b[:], 8, tab2_scales[2:3])
        load_scales_side_by_side(ws_raw[:, 0 : 3 * H], 0, w2_scales)
        load_scales_side_by_side(ws_raw[:, 3 * H : 4 * H], 0, w4_scales)
        b4_t = keep.tile([P, PACK], F32, name="b4_t")
        nc.sync.dma_start(b4_t[:], b4.rearrange("(p t) -> p t", t=PACK))
        tab_a0 = load_table_pass(tab_words, 0, "tab_a0")
        w1_raw.append(load_rows(w1[K_PASS : 2 * K_PASS, :], "w1_raw1"))
        tab_a1 = load_table_pass(tab_words, 1, "tab_a1")
        w3_raw = load_rows(w3, "w3_raw")
        tab_d = load_table_pass(tab3_words, 0, "tab_d")
        w2_raw = keep.tile([P, 3, 2 * H], U8, name="w2_raw")
        nc.sync.dma_start(w2_raw[:].bitcast(I32), w2_words.bitcast(I32).rearrange("a p c -> p a c"))

        def e4m3_columns(codes):
            return lambda t: codes[:, t * P : (t + 1) * P].bitcast(FP8X4)

        def e2m1_columns(a):
            return lambda t: w2[:, (a * H + t * P) * 2 : (a * H + (t + 1) * P) * 2].bitcast(FP4X4)

        def pick_a(t):
            nc.vector.tensor_copy(aj[:, t, :], res_a[t][:].indirect(p_a[:]))

        def pick_d(t):
            nc.vector.tensor_tensor(da[:, t, :], res_d[t][:].indirect(p_d[:]), aj[:, t, :], ALU.subtract)

        s_a = gather_scales(win_a, l_a, "s_a")
        s_d = gather_scales(win_d, l_d, "s_d")
        w1_q = [quantize(weave_dealt(w1_raw[0], "w1_woven0"), H, "w1_0")]
        s_b = gather_scales(win_b, l_b, "s_b")
        ws = keep.tile([P, 4 * H], U8, name="ws", align_bytes=64)
        nc.vector.tensor_copy(
            ws[:].rearrange("p (a t m) -> p a t m", a=4, t=PACK), ws_raw[:].rearrange("p (a m t) -> p a t m", a=4, t=PACK)
        )
        g_a0 = gather_words(tab_a0, l_a, 0, S, "g_a0", "g_a0", 1)
        move_up(s_b1, s_b, 16)
        move_up(s_b2, s_b, 8)
        tab_b = [load_table_pass(tab2_words, 0, "tab_b0")]
        w1_q.append(quantize(weave_dealt(w1_raw[1], "w1_woven1"), H, "w1_1"))
        banks = new_banks("acc_a")
        first_stage_pass(banks, e4m3_columns(w1_q[0][0]), w1_q[0][1], halves(g_a0), s_a[4:P, :], True, False)
        g_a1 = [gather_words(tab_a1, l_a, n * HALF, HALF, "g_a1%d" % n, "woven", 2)[:] for n in range(2)]
        first_stage_pass(banks, e4m3_columns(w1_q[1][0]), w1_q[1][1], g_a1, s_a[8:P, :], False, True)
        tab_b.append(load_table_pass(tab2_words, 1, "tab_b1"))
        res_a = new_results("a", "ab")
        empty_banks(res_a, banks)
        aj = keep.tile([P, PACK, J], F32, name="aj")
        for t in range(PACK - 1):
            pick_a(t)

        w3_woven = weave_dealt(w3_raw, "w3_woven")
        g_d = [gather_words(tab_d, l_d, 0, HALF, "g_d0", "ab2", 1)[:]]
        w3_q = quantize(w3_woven, H, "w3")
        g_d.append(gather_words(tab_d, l_d, HALF, HALF, "g_d1", "ab1", 1)[:])
        pick_a(PACK - 1)
        banks = new_banks("acc_d")
        first_stage_pass(banks, e4m3_columns(w3_q[0]), w3_q[1], g_d, s_d[12:P, :], True, True)
        tab_b.append(load_table_pass(tab2_words, 2, "tab_b2"))
        w2 = ring.tile([P, 3 * 2 * H], U8, tag="woven", bufs=2, name="w2", align_bytes=64)
        nc.scalar.copy(
            w2[:].bitcast(U16).rearrange("p (a t m) -> p a t m", a=3, t=PACK),
            w2_raw[:].bitcast(U16).rearrange("p a (m t) -> p a t m", t=PACK),
        )
        res_d = new_results("d", "dh")
        empty_banks(res_d, banks)

        da = keep.tile([P, PACK, J], F32, name="da")
        banks = new_banks("acc_b")

        def b_pass(a, picked, plane):
            first_stage_pass(banks, e2m1_columns(a), ws[:, a * H : (a + 1) * H], picked, plane, a == 0, a == 2)

        pick_d(0)
        g_b0 = gather_words(tab_b[0], l_b, 0, S, "g_b0", "dh0", 1)
        b_pass(0, halves(g_b0), s_b)
        w4_raw = ring.tile([P, H], I32, tag="table", bufs=3, name="w4_raw")
        nc.sync.dma_start(w4_raw[:], w4_words[0].rearrange("p c i -> p (c i)").bitcast(I32))
        pick_d(1)
        g_b1 = gather_words(tab_b[1], l_b, 0, S, "g_b1", "dh1", 1)
        b_pass(1, halves(g_b1), s_b1)
        w5_raw = ring.tile([P, PACK, N_OUT], F32, tag="table", bufs=3, name="w5_raw")
        nc.sync.dma_start(w5_raw[:], w5.rearrange("(p j) c -> p j c", j=PACK))
        pick_d(2)
        g_b2 = [gather_words(tab_b[2], l_b, n * HALF, HALF, "g_b2%d" % n, ("dh2", "dh0")[n], 1)[:] for n in range(2)]
        b_pass(2, g_b2, s_b2)
        pick_d(3)
        res_b = new_results("b", "ab")
        empty_banks(res_b, banks)
        w4 = keep.tile([P, H], U32, name="w4", align_bytes=64)
        nc.scalar.copy(
            w4[:].rearrange("p (t m) -> p m t", t=PACK), w4_raw[:].bitcast(U32).rearrange("p (m t) -> p m t", t=PACK)
        )

        z = keep.tile([P, PACK, J], F32, name="z")

        def difference(piece, t, tag):
            first, width = piece
            ba = ring.tile([P, width], F32, tag=tag, bufs=1, name="ba%d_%d" % (first, t), align_bytes=64)
            offsets = p_b[:, first // 16 : (first + width) // 16]
            nc.vector.tensor_tensor(ba[:], res_b[t][:].indirect(offsets), aj[:, t, first : first + width], ALU.subtract)
            return ba

        def product(piece, t, ba):
            cols = slice(piece[0], piece[0] + piece[1])
            nc.vector.scalar_tensor_tensor(z[:, t, cols], ba[:], gain_t[:, t : t + 1], da[:, t, cols], ALU.mult, ALU.mult)

        def weave_z(piece):
            first, width = piece
            return weave(nc.scalar.copy, z[:, :, first : first + width], width, "z_woven%d" % first)

        def hidden(piece, z_woven):
            first, width = piece
            codes, scales = quantize(z_woven, width, "z%d" % first)
            ys = []
            for t in range(PACK):
                y = psum.tile([P, width], F32, tag="bank", name="y%d_%d" % (first, t))
                nc.tensor.matmul_mx(
                    out=y[:],
                    lhsT=w4[:, t * P : (t + 1) * P].bitcast(FP8X4),
                    lhsT_scale=ws[:, 3 * H + t * P : 3 * H + (t + 1) * P],
                    rhs=codes[:].bitcast(FP8X4),
                    rhs_scale=scales[:],
                    start=True,
                    stop=True,
                )
                ys.append(y)
            return ys

        def larger(piece, ys, mover, tag):
            first, width = piece
            cols = slice(first, first + width)
            hid = ring.tile([P, PACK, width], F32, tag=tag, bufs=1, name="h%d" % first, align_bytes=64)
            for t in range(PACK):
                nc.vector.scalar_tensor_tensor(hid[:, t, :], ys[t][:], b4_t[:, t : t + 1], z[:, t, cols], ALU.add, ALU.max)
            return weave(mover, hid[:], width, "h_woven%d" % first)

        def scores(piece, h_woven, movers, tag):
            first, width = piece
            codes, scales = quantize(h_woven, width, "h%d" % first)
            staged = ring.tile([P, N_OUT // P, width], F32, tag=tag, bufs=1, name="staged%d" % first, align_bytes=64)
            for n in range(N_OUT // P):
                acc = psum.tile([P, width], F32, tag="bank", name="o%d_%d" % (first, n))
                nc.tensor.matmul_mx(
                    out=acc[:],
                    lhsT=w5_q[0][:, n * P : (n + 1) * P].bitcast(FP8X4),
                    lhsT_scale=w5_q[1][:, n * P : (n + 1) * P],
                    rhs=codes[:].bitcast(FP8X4),
                    rhs_scale=scales[:],
                    start=True,
                    stop=True,
                )
                movers[n](staged[:, n, :], acc[:])
                nc.sync.dma_start(out[n * P : (n + 1) * P, first : first + width], staged[:, n, :])

        one, two = PIECES
        ba0 = difference(one, 0, "ba_even")
        ba1 = difference(one, 1, "ba_odd")
        product(one, 0, ba0)
        early = difference(two, 0, "ba_early")
        product(one, 1, ba1)
        ba2 = difference(one, 2, "ba_even")
        product(two, 0, early)
        ba3 = difference(one, 3, "ba_odd")
        product(one, 2, ba2)
        product(one, 3, ba3)
        z0 = weave_z(one)
        w5_woven = keep.tile([P, PACK * N_OUT], BF16, name="w5_woven", align_bytes=64)
        nc.scalar.copy(
            w5_woven[:].rearrange("p (c i t) -> p c t i", t=PACK, i=4), w5_raw[:].rearrange("p t (c i) -> p c t i", i=4)
        )
        ba1 = difference(two, 1, "ba_odd")
        ba3 = difference(two, 3, "ba_even")
        product(two, 1, ba1)
        y0 = hidden(one, z0)
        ba2 = difference(two, 2, "z_woven0")
        product(two, 3, ba3)
        product(two, 2, ba2)
        z1 = weave_z(two)
        h0 = larger(one, y0, nc.scalar.copy, "dh2")
        w5_q = quantize(w5_woven, N_OUT, "w5")
        y1 = hidden(two, z1)
        scores(one, h0, [nc.scalar.copy] * 3, "dh0")
        h1 = larger(two, y1, nc.vector.tensor_copy, "dh1")
        scores(two, h1, [nc.scalar.copy, nc.vector.tensor_copy, nc.scalar.copy], "dh3")
